import numpy as np
import ml_dtypes


def mxq(x, axis, fmt="e4m3"):
    dtype, down = {"e4m3": (ml_dtypes.float8_e4m3fn, 7), "e5m2": (ml_dtypes.float8_e5m2, 14)}[fmt]
    v = np.moveaxis(np.asarray(x, np.float32).astype(ml_dtypes.bfloat16).astype(np.float64), axis, -1)
    blocks = v.reshape(v.shape[:-1] + (-1, 32))
    amax = np.abs(blocks).max(-1, keepdims=True)
    byte = np.maximum(np.where(amax > 0, np.frexp(amax)[1] - 1 + 127, 0) - down, 1)
    scale = np.exp2(byte - 127.0)
    codes = (blocks / scale).astype(np.float32).astype(dtype).astype(np.float64)
    return np.moveaxis((codes * scale).reshape(v.shape), -1, axis)


WIDE = False


def mx_kscale(k):
    if not WIDE:
        return np.ones(k)
    levels = np.array([10, -10, 5, -5, 0])
    if k % 512:
        return np.exp2(np.random.permutation(np.resize(levels, k // 32))).repeat(32)
    a = np.empty((k // 512, 16))
    for p in range(k // 512):
        a[p, :8] = np.random.permutation(np.resize(levels, 8))
        for g in range(8):
            far = levels[np.abs(levels - a[p, g]) >= 10]
            a[p, g + 8] = far[np.random.randint(len(far))]
    return np.exp2(a.ravel()).repeat(32)


def f64(x):
    return np.asarray(x).astype(np.float64)


def striped(idx):
    return np.tile(idx.reshape(-1, 16).T, (8, 1)).astype(np.uint16)


def unstriped(offs):
    return offs[:16].T.reshape(-1).astype(np.int64)


def striped8(idx):
    return np.concatenate([x.reshape(-1, 16).T for x in idx]).astype(np.uint16)


def runs(offs, k):
    lists = np.stack([offs[16 * r : 16 * r + 16].T.reshape(-1) for r in range(8)]).astype(np.int64)
    return lists[np.arange(k) % 512 // 64]


def pack_weight(w):
    k, n = w.shape
    w = f64(np.asarray(w, np.float32).astype(ml_dtypes.bfloat16)).reshape(k // 32, 32, n)
    amax = np.abs(w).max(1)
    byte = np.clip(np.where(amax > 0, np.frexp(amax)[1] - 1 + 127 - 7, 1), 1, 254)
    scaled = (w * np.exp2(127.0 - byte)[:, None, :]).reshape(k, n).astype(np.float32)
    words = np.ascontiguousarray(scaled.reshape(k // 512, 128, 4, n).transpose(0, 1, 3, 2)).astype(ml_dtypes.float8_e4m3fn).view(np.uint8)
    return words, np.ascontiguousarray(byte.astype(np.uint8).reshape(k // 512, 16, n))


def unpack_weight(words, scales):
    g, p, n, _ = words.shape
    vals = np.ascontiguousarray(words).view(ml_dtypes.float8_e4m3fn).astype(np.float64) * np.repeat(np.exp2(scales.astype(np.float64) - 127.0), 8, axis=1)[..., None]
    return vals.transpose(0, 1, 3, 2).reshape(g * 512, n)


def relu(v):
    return np.maximum(v, 0.0)


K, T, S, G, H, C = 512, 2048, 512, 2048, 512, 512


def setup_inputs():
    n = np.random.standard_normal
    s = mx_kscale(K)[:, None]
    packed_xT = pack_weight(n((K, T)) * s)
    packed_dT = pack_weight(n((K, G)) / s)
    return {
        "x_words": packed_xT[0],
        "x_scales": packed_xT[1],
        "d_words": packed_dT[0],
        "d_scales": packed_dT[1],
        "gs": (np.random.uniform(0.5, 1.5, (K, 1)) / s).astype(np.float32),
        "offs": striped(np.random.permutation(T)[:S]),
        "k1": striped8(np.random.randint(0, G, (8, H))),
        "nb": striped8(np.stack([np.random.permutation(S) for _ in range(8)])),
        "cand": striped(np.random.permutation(T)[:C]),
    }


def reference(x_words, x_scales, d_words, d_scales, gs, offs, k1, nb, cand):
    x_cand = unpack_weight(x_words, x_scales)[:, unstriped(cand)]
    d_k1 = unpack_weight(d_words, d_scales)[np.arange(K)[:, None], runs(k1, K)]
    xq = unpack_weight(x_words, x_scales)[:, unstriped(offs)]
    h = 0.0625 * (d_k1.T @ xq)
    z = f64(gs) * (relu(h - (h[np.arange(H)[:, None], runs(nb, H)])))
    s = 0.0625 * ((x_cand.T @ mxq(z, 0, "e4m3")))
    return s

@@ -1,0 +1,134 @@
+from contextlib import ExitStack
+
+import concourse.mybir as mybir
+
+K, T, S, G, H, C = 512, 2048, 512, 2048, 512, 512
+FLOPS = 2 * K * H * S + 2 * K * C * S
+
+F32 = mybir.dt.float32
+BF16 = mybir.dt.bfloat16
+I32 = mybir.dt.int32
+U32 = mybir.dt.uint32
+U16 = mybir.dt.uint16
+U8 = mybir.dt.uint8
+FP8X4 = mybir.dt.float8_e4m3fn_x4
+ALU = mybir.AluOpType
+COPY = mybir.ActivationFunctionType.Copy
+
+P = 128
+PACK = 4
+CHUNKS = [256, 128, 128]
+
+
+def tile_picked_pqcand_none_p_kernel(tc, x_words, x_scales, d_words, d_scales, gs, offs, k1, nb, cand, out):
+    nc = tc.nc
+    with ExitStack() as ctx:
+        keep = ctx.enter_context(tc.tile_pool(name="keep", bufs=1))
+        psum = ctx.enter_context(tc.psum_pool(name="psum", bufs=1))
+
+        k1_sb = keep.tile([P, H // 16], U16, name="k1_sb")
+        offs_sb = keep.tile([P, S // 16], U16, name="offs_sb")
+        cand_sb = keep.tile([P, C // 16], U16, name="cand_sb")
+        nb_sb = keep.tile([P, S // 16], U16, name="nb_sb")
+        d_word_table = keep.tile([P, G], U32, name="d_word_table", align_bytes=64)
+        x_word_table = keep.tile([P, T], U32, name="x_word_table", align_bytes=64)
+        d_byte_table = keep.tile([P, G], U8, name="d_byte_table", align_bytes=64)
+        x_byte_table = keep.tile([P, T], U8, name="x_byte_table", align_bytes=64)
+        d_bytes = keep.tile([P, H], U8, name="d_bytes", align_bytes=64)
+        gain = keep.tile([P, PACK], F32, name="gain")
+
+        nc.vector.memset(d_byte_table[:].bitcast(I32), 0)
+        nc.gpsimd.memset(x_byte_table[:].bitcast(I32), 0)
+        nc.gpsimd.memset(d_bytes[:].bitcast(I32), 0)
+
+        nc.sync.dma_start(k1_sb[:], k1)
+        nc.scalar.dma_start(d_byte_table[0:P:8, :].bitcast(I32), d_scales[0].bitcast(I32))
+        nc.sync.dma_start(offs_sb[:], offs)
+        nc.sync.dma_start(d_word_table[:].bitcast(I32), d_words[0].rearrange("p n t -> p (n t)").bitcast(I32))
+        for s in range(4):
+            nc.scalar.dma_start(x_byte_table[s:P:32, :].bitcast(I32), x_scales[0, s:16:4, :].bitcast(I32))
+        nc.sync.dma_start(x_word_table[:].bitcast(I32), x_words[0].rearrange("p n t -> p (n t)").bitcast(I32))
+        nc.sync.dma_start(cand_sb[:], cand)
+        nc.sync.dma_start(nb_sb[:], nb)
+        nc.sync.dma_start(gain[:], gs.rearrange("(p t) o -> p (t o)", t=PACK))
+
+        d_bytes_listed = keep.tile([P, H], U8, name="d_bytes_listed", align_bytes=64)
+        nc.vector.tensor_copy(d_bytes_listed[:], d_byte_table[:].indirect(k1_sb[:]))
+        d_bytes_dealt = keep.tile([P, H], U8, name="d_bytes_dealt", align_bytes=64)
+        nc.vector.tensor_copy(
+            d_bytes_dealt[:].rearrange("p (t c i) -> p c t i", t=PACK, i=16),
+            d_bytes_listed[:].rearrange("p (c i t) -> p c t i", t=PACK, i=16),
+        )
+        for s in range(4):
+            nc.scalar.dma_start(d_bytes[s:P:32, :].bitcast(I32), d_bytes_dealt[8 * s : P : 32, :].bitcast(I32))
+
+        xq_bytes = keep.tile([P, S], U8, name="xq_bytes", align_bytes=64)
+        nc.vector.tensor_copy(xq_bytes[:], x_byte_table[:].indirect(offs_sb[:]))
+        d_codes_listed = keep.tile([P, H], U32, name="d_codes_listed", align_bytes=64)
+        nc.vector.tensor_copy(d_codes_listed[:], d_word_table[:].indirect(k1_sb[:]))
+        d_codes = keep.tile([P, H], U32, name="d_codes", align_bytes=64)
+        nc.vector.tensor_copy(
+            d_codes[:].rearrange("p (t c i) -> p c t i", t=PACK, i=4),
+            d_codes_listed[:].rearrange("p (c i t) -> p c t i", t=PACK, i=4),
+        )
+        xq_codes = keep.tile([P, S], U32, name="xq_codes", align_bytes=64)
+        nc.vector.tensor_copy(xq_codes[:], x_word_table[:].indirect(offs_sb[:]))
+        xc_bytes = keep.tile([P, C], U8, name="xc_bytes", align_bytes=64)
+        nc.vector.tensor_copy(xc_bytes[:], x_byte_table[:].indirect(cand_sb[:]))
+        xc_codes = keep.tile([P, C], U32, name="xc_codes", align_bytes=64)
+        nc.vector.tensor_copy(xc_codes[:], x_word_table[:].indirect(cand_sb[:]))
+
+        first = CHUNKS[0]
+        window, head, rest = [], [], []
+        for t in range(PACK):
+            cols = slice(t * P, (t + 1) * P)
+            acc = psum.tile([P, S], F32, name=f"h_acc{t}")
+            nc.tensor.matmul_mx(
+                out=acc[:],
+                lhsT=d_codes[:, cols].bitcast(FP8X4),
+                lhsT_scale=d_bytes[:, cols],
+                rhs=xq_codes[:].bitcast(FP8X4),
+                rhs_scale=xq_bytes[:],
+                start=True,
+                stop=True,
+            )
+            window.append(keep.tile([P, S], F32, name=f"window{t}"))
+            head.append(keep.tile([P, first], F32, name=f"head{t}"))
+            rest.append(keep.tile([P, S - first], F32, name=f"rest{t}"))
+            nc.scalar.activation(window[t][:], acc[:], COPY, scale=-0.0625)
+            nc.scalar.activation(head[t][:], acc[:, :first], COPY, scale=-0.0625)
+            nc.sync.dma_start(rest[t][:], window[t][:, first:])
+
+        out_tiles = out.rearrange("(m p) j -> p m j", p=P)
+        j0 = 0
+        for u, n in enumerate(CHUNKS):
+            planes = keep.tile([P, PACK, n], BF16, name=f"planes{u}", align_bytes=64)
+            for t in range(PACK):
+                own = head[t][:] if u == 0 else rest[t][:, j0 - first : j0 - first + n]
+                diff = keep.tile([P, n], F32, name=f"diff{u}_{t}")
+                nc.vector.tensor_tensor(diff[:], window[t][:].indirect(nb_sb[:, j0 // 16 : (j0 + n) // 16]), own, ALU.subtract)
+                nc.vector.tensor_scalar(planes[:, t, :], diff[:], 0.0, gain[:, t : t + 1], ALU.max, ALU.mult)
+            woven = keep.tile([P, n, PACK], BF16, name=f"woven{u}", align_bytes=64)
+            nc.scalar.copy(woven[:].rearrange("p (c i) t -> p c t i", i=4), planes[:].rearrange("p t (c i) -> p c t i", i=4))
+            z_codes = keep.tile([P, n], U32, name=f"z_codes{u}", align_bytes=64)
+            z_bytes = keep.tile([P, n], U8, name=f"z_bytes{u}", align_bytes=64)
+            nc.vector.quantize_mx(out=z_codes[:].bitcast(FP8X4), scales=z_bytes[:], in_=woven[:].rearrange("p j t -> p (j t)"))
+            per_bank = 512 // n
+            for b in range(C // P // per_bank):
+                acc = psum.tile([P, per_bank, n], F32, name=f"s_acc{u}_{b}")
+                for i in range(per_bank):
+                    m = b * per_bank + i
+                    cols = slice(m * P, (m + 1) * P)
+                    nc.tensor.matmul_mx(
+                        out=acc[:, i, :],
+                        lhsT=xc_codes[:, cols].bitcast(FP8X4),
+                        lhsT_scale=xc_bytes[:, cols],
+                        rhs=z_codes[:].bitcast(FP8X4),
+                        rhs_scale=z_bytes[:],
+                        start=True,
+                        stop=True,
+                    )
+                staged = keep.tile([P, per_bank, n], F32, name=f"staged{u}_{b}")
+                nc.scalar.activation(staged[:], acc[:], COPY, scale=0.0625)
+                nc.sync.dma_start(out_tiles[:, b * per_bank : (b + 1) * per_bank, j0 : j0 + n], staged[:])
+            j0 += n

@@ -17,7 +17,11 @@ COPY = mybir.ActivationFunctionType.Copy
 
 P = 128
 PACK = 4
+D_FIRST = 1024
+CLEAR_SPLIT = 1280
 CHUNKS = [256, 128, 128]
+BANKS = [["s0", "s1"], ["s2"], ["s3", "h0"]]
+TAIL_SCALAR = 48
 
 
 def tile_picked_pqcand_none_p_kernel(tc, x_words, x_scales, d_words, d_scales, gs, offs, k1, nb, cand, out):
@@ -37,20 +41,23 @@ def tile_picked_pqcand_none_p_kernel(tc, x_words, x_scales, d_words, d_scales, g
         d_bytes = keep.tile([P, H], U8, name="d_bytes", align_bytes=64)
         gain = keep.tile([P, PACK], F32, name="gain")
 
-        nc.vector.memset(d_byte_table[:].bitcast(I32), 0)
-        nc.gpsimd.memset(x_byte_table[:].bitcast(I32), 0)
-        nc.gpsimd.memset(d_bytes[:].bitcast(I32), 0)
+        for table in (d_byte_table, x_byte_table):
+            nc.vector.memset(table[:, :CLEAR_SPLIT].bitcast(I32), 0)
+            nc.gpsimd.memset(table[:, CLEAR_SPLIT:].bitcast(I32), 0)
+        nc.vector.memset(d_bytes[:].bitcast(I32), 0)
 
+        d_rows = d_words[0].rearrange("p n t -> p (n t)").bitcast(I32)
         nc.sync.dma_start(k1_sb[:], k1)
         nc.scalar.dma_start(d_byte_table[0:P:8, :].bitcast(I32), d_scales[0].bitcast(I32))
         nc.sync.dma_start(offs_sb[:], offs)
-        nc.sync.dma_start(d_word_table[:].bitcast(I32), d_words[0].rearrange("p n t -> p (n t)").bitcast(I32))
+        nc.sync.dma_start(nb_sb[:], nb)
+        nc.sync.dma_start(gain[:], gs.rearrange("(p t) o -> p (t o)", t=PACK))
+        nc.sync.dma_start(d_word_table[:, :D_FIRST].bitcast(I32), d_rows[:, :D_FIRST])
+        nc.sync.dma_start(d_word_table[:, D_FIRST:].bitcast(I32), d_rows[:, D_FIRST:])
         for s in range(4):
             nc.scalar.dma_start(x_byte_table[s:P:32, :].bitcast(I32), x_scales[0, s:16:4, :].bitcast(I32))
         nc.sync.dma_start(x_word_table[:].bitcast(I32), x_words[0].rearrange("p n t -> p (n t)").bitcast(I32))
         nc.sync.dma_start(cand_sb[:], cand)
-        nc.sync.dma_start(nb_sb[:], nb)
-        nc.sync.dma_start(gain[:], gs.rearrange("(p t) o -> p (t o)", t=PACK))
 
         d_bytes_listed = keep.tile([P, H], U8, name="d_bytes_listed", align_bytes=64)
         nc.vector.tensor_copy(d_bytes_listed[:], d_byte_table[:].indirect(k1_sb[:]))
@@ -62,8 +69,6 @@ def tile_picked_pqcand_none_p_kernel(tc, x_words, x_scales, d_words, d_scales, g
         for s in range(4):
             nc.scalar.dma_start(d_bytes[s:P:32, :].bitcast(I32), d_bytes_dealt[8 * s : P : 32, :].bitcast(I32))
 
-        xq_bytes = keep.tile([P, S], U8, name="xq_bytes", align_bytes=64)
-        nc.vector.tensor_copy(xq_bytes[:], x_byte_table[:].indirect(offs_sb[:]))
         d_codes_listed = keep.tile([P, H], U32, name="d_codes_listed", align_bytes=64)
         nc.vector.tensor_copy(d_codes_listed[:], d_word_table[:].indirect(k1_sb[:]))
         d_codes = keep.tile([P, H], U32, name="d_codes", align_bytes=64)
@@ -73,18 +78,84 @@ def tile_picked_pqcand_none_p_kernel(tc, x_words, x_scales, d_words, d_scales, g
         )
         xq_codes = keep.tile([P, S], U32, name="xq_codes", align_bytes=64)
         nc.vector.tensor_copy(xq_codes[:], x_word_table[:].indirect(offs_sb[:]))
+        xq_bytes = keep.tile([P, S], U8, name="xq_bytes", align_bytes=64)
+        nc.vector.tensor_copy(xq_bytes[:], x_byte_table[:].indirect(offs_sb[:]))
         xc_bytes = keep.tile([P, C], U8, name="xc_bytes", align_bytes=64)
         nc.vector.tensor_copy(xc_bytes[:], x_byte_table[:].indirect(cand_sb[:]))
         xc_codes = keep.tile([P, C], U32, name="xc_codes", align_bytes=64)
         nc.vector.tensor_copy(xc_codes[:], x_word_table[:].indirect(cand_sb[:]))
 
-        first = CHUNKS[0]
-        window, head, rest = [], [], []
+        starts = [sum(CHUNKS[:u]) for u in range(len(CHUNKS))]
+        h_acc, window, own, planes, woven, s_acc = [], [], {}, {}, {}, {}
+        out_tiles = out.rearrange("(m p) j -> p m j", p=P)
+
+        def copy_own(u, t):
+            own[u, t] = keep.tile([P, CHUNKS[u]], F32, name=f"own{u}_{t}")
+            nc.scalar.activation(own[u, t][:], h_acc[t][:, starts[u] : starts[u] + CHUNKS[u]], COPY, scale=-0.0625)
+
+        def fetch(u):
+            n, j0 = CHUNKS[u], starts[u]
+            planes[u] = keep.tile([P, PACK, n], BF16, name=f"planes{u}", align_bytes=64)
+            diff = keep.tile([P, PACK, n], F32, name=f"diff{u}", tag=f"turn{u % 2}", align_bytes=64)
+            for t in range(PACK + 1):
+                if t < PACK:
+                    nc.vector.tensor_tensor(
+                        diff[:, t, :], window[t][:].indirect(nb_sb[:, j0 // 16 : (j0 + n) // 16]), own[u, t][:], ALU.subtract
+                    )
+                if t > 0:
+                    nc.vector.tensor_scalar(planes[u][:, t - 1, :], diff[:, t - 1, :], 0.0, gain[:, t - 1 : t], ALU.max, ALU.mult)
+
+        def weave(u):
+            woven[u] = keep.tile([P, CHUNKS[u], PACK], BF16, name=f"woven{u}", tag=f"turn{u % 2}", align_bytes=64)
+            n = CHUNKS[u]
+            cut = n if u < len(CHUNKS) - 1 else TAIL_SCALAR
+            nc.scalar.copy(
+                woven[u][:, :cut, :].rearrange("p (c i) t -> p c t i", i=4),
+                planes[u][:, :, :cut].rearrange("p t (c i) -> p c t i", i=4),
+            )
+            if cut < n:
+                nc.vector.tensor_copy(
+                    woven[u][:, cut:, :].rearrange("p (c i) t -> p c t i", i=4),
+                    planes[u][:, :, cut:].rearrange("p t (c i) -> p c t i", i=4),
+                )
+
+        def score(u, tags):
+            n = CHUNKS[u]
+            z_codes = keep.tile([P, n], U32, name=f"z_codes{u}", align_bytes=64)
+            z_bytes = keep.tile([P, n], U8, name=f"z_bytes{u}", align_bytes=64)
+            nc.vector.quantize_mx(out=z_codes[:].bitcast(FP8X4), scales=z_bytes[:], in_=woven[u][:].rearrange("p j t -> p (j t)"))
+            per_bank = C // P // len(tags)
+            s_acc[u] = [psum.tile([P, per_bank, n], F32, name=f"s_acc{u}_{b}", tag=tag) for b, tag in enumerate(tags)]
+            for m in range(C // P):
+                cols = slice(m * P, (m + 1) * P)
+                nc.tensor.matmul_mx(
+                    out=s_acc[u][m // per_bank][:, m % per_bank, :],
+                    lhsT=xc_codes[:, cols].bitcast(FP8X4),
+                    lhsT_scale=xc_bytes[:, cols],
+                    rhs=z_codes[:].bitcast(FP8X4),
+                    rhs_scale=z_bytes[:],
+                    start=True,
+                    stop=True,
+                )
+
+        def store(u):
+            n, j0 = CHUNKS[u], starts[u]
+            per_bank = C // P // len(s_acc[u])
+            for b, acc in enumerate(s_acc[u]):
+                staged = keep.tile([P, per_bank, n], F32, name=f"staged{u}_{b}")
+                target = out_tiles[:, b * per_bank : (b + 1) * per_bank, j0 : j0 + n]
+                if b == 0 or u < len(CHUNKS) - 1:
+                    nc.scalar.activation(staged[:], acc[:], COPY, scale=0.0625)
+                    nc.sync.dma_start(target, staged[:])
+                else:
+                    nc.vector.tensor_scalar(staged[:], acc[:], 0.0625, None, ALU.mult)
+                    nc.scalar.dma_start(target, staged[:])
+
         for t in range(PACK):
             cols = slice(t * P, (t + 1) * P)
-            acc = psum.tile([P, S], F32, name=f"h_acc{t}")
+            h_acc.append(psum.tile([P, S], F32, name=f"h_acc{t}", tag=f"h{t}"))
             nc.tensor.matmul_mx(
-                out=acc[:],
+                out=h_acc[t][:],
                 lhsT=d_codes[:, cols].bitcast(FP8X4),
                 lhsT_scale=d_bytes[:, cols],
                 rhs=xq_codes[:].bitcast(FP8X4),
@@ -93,42 +164,19 @@ def tile_picked_pqcand_none_p_kernel(tc, x_words, x_scales, d_words, d_scales, g
                 stop=True,
             )
             window.append(keep.tile([P, S], F32, name=f"window{t}"))
-            head.append(keep.tile([P, first], F32, name=f"head{t}"))
-            rest.append(keep.tile([P, S - first], F32, name=f"rest{t}"))
-            nc.scalar.activation(window[t][:], acc[:], COPY, scale=-0.0625)
-            nc.scalar.activation(head[t][:], acc[:, :first], COPY, scale=-0.0625)
-            nc.sync.dma_start(rest[t][:], window[t][:, first:])
+            nc.scalar.activation(window[t][:], h_acc[t][:], COPY, scale=-0.0625)
+            copy_own(0, t)
 
-        out_tiles = out.rearrange("(m p) j -> p m j", p=P)
-        j0 = 0
-        for u, n in enumerate(CHUNKS):
-            planes = keep.tile([P, PACK, n], BF16, name=f"planes{u}", align_bytes=64)
-            for t in range(PACK):
-                own = head[t][:] if u == 0 else rest[t][:, j0 - first : j0 - first + n]
-                diff = keep.tile([P, n], F32, name=f"diff{u}_{t}")
-                nc.vector.tensor_tensor(diff[:], window[t][:].indirect(nb_sb[:, j0 // 16 : (j0 + n) // 16]), own, ALU.subtract)
-                nc.vector.tensor_scalar(planes[:, t, :], diff[:], 0.0, gain[:, t : t + 1], ALU.max, ALU.mult)
-            woven = keep.tile([P, n, PACK], BF16, name=f"woven{u}", align_bytes=64)
-            nc.scalar.copy(woven[:].rearrange("p (c i) t -> p c t i", i=4), planes[:].rearrange("p t (c i) -> p c t i", i=4))
-            z_codes = keep.tile([P, n], U32, name=f"z_codes{u}", align_bytes=64)
-            z_bytes = keep.tile([P, n], U8, name=f"z_bytes{u}", align_bytes=64)
-            nc.vector.quantize_mx(out=z_codes[:].bitcast(FP8X4), scales=z_bytes[:], in_=woven[:].rearrange("p j t -> p (j t)"))
-            per_bank = 512 // n
-            for b in range(C // P // per_bank):
-                acc = psum.tile([P, per_bank, n], F32, name=f"s_acc{u}_{b}")
-                for i in range(per_bank):
-                    m = b * per_bank + i
-                    cols = slice(m * P, (m + 1) * P)
-                    nc.tensor.matmul_mx(
-                        out=acc[:, i, :],
-                        lhsT=xc_codes[:, cols].bitcast(FP8X4),
-                        lhsT_scale=xc_bytes[:, cols],
-                        rhs=z_codes[:].bitcast(FP8X4),
-                        rhs_scale=z_bytes[:],
-                        start=True,
-                        stop=True,
-                    )
-                staged = keep.tile([P, per_bank, n], F32, name=f"staged{u}_{b}")
-                nc.scalar.activation(staged[:], acc[:], COPY, scale=0.0625)
-                nc.sync.dma_start(out_tiles[:, b * per_bank : (b + 1) * per_bank, j0 : j0 + n], staged[:])
-            j0 += n
+        last = len(CHUNKS) - 1
+        for u in range(last + 3):
+            if u <= last:
+                fetch(u)
+            if u + 1 <= last:
+                for t in range(PACK):
+                    copy_own(u + 1, t)
+            if 1 <= u <= last + 1:
+                score(u - 1, BANKS[u - 1])
+            if u <= last:
+                weave(u)
+            if 1 <= u <= last + 1:
+                store(u - 1)

@@ -20,7 +20,7 @@ PACK = 4
 D_FIRST = 1024
 CLEAR_SPLIT = 1280
 CHUNKS = [256, 128, 128]
-BANKS = [["s0", "s1"], ["s2"], ["s3", "h0"]]
+BANKS = [["s0", "s1"], ["s2"], ["s3", "h0", "h1", "h2"]]
 TAIL_SCALAR = 48
 
 
@@ -38,17 +38,16 @@ def tile_picked_pqcand_none_p_kernel(tc, x_words, x_scales, d_words, d_scales, g
         x_word_table = keep.tile([P, T], U32, name="x_word_table", align_bytes=64)
         d_byte_table = keep.tile([P, G], U8, name="d_byte_table", align_bytes=64)
         x_byte_table = keep.tile([P, T], U8, name="x_byte_table", align_bytes=64)
-        d_bytes = keep.tile([P, H], U8, name="d_bytes", align_bytes=64)
         gain = keep.tile([P, PACK], F32, name="gain")
 
         for table in (d_byte_table, x_byte_table):
             nc.vector.memset(table[:, :CLEAR_SPLIT].bitcast(I32), 0)
             nc.gpsimd.memset(table[:, CLEAR_SPLIT:].bitcast(I32), 0)
-        nc.vector.memset(d_bytes[:].bitcast(I32), 0)
 
         d_rows = d_words[0].rearrange("p n t -> p (n t)").bitcast(I32)
         nc.sync.dma_start(k1_sb[:], k1)
-        nc.scalar.dma_start(d_byte_table[0:P:8, :].bitcast(I32), d_scales[0].bitcast(I32))
+        for e in range(2):
+            nc.scalar.dma_start(d_byte_table[e:P:16, :].bitcast(I32), d_scales[0, e:16:2, :].bitcast(I32))
         nc.sync.dma_start(offs_sb[:], offs)
         nc.sync.dma_start(nb_sb[:], nb)
         nc.sync.dma_start(gain[:], gs.rearrange("(p t) o -> p (t o)", t=PACK))
@@ -61,25 +60,24 @@ def tile_picked_pqcand_none_p_kernel(tc, x_words, x_scales, d_words, d_scales, g
 
         d_bytes_listed = keep.tile([P, H], U8, name="d_bytes_listed", align_bytes=64)
         nc.vector.tensor_copy(d_bytes_listed[:], d_byte_table[:].indirect(k1_sb[:]))
-        d_bytes_dealt = keep.tile([P, H], U8, name="d_bytes_dealt", align_bytes=64)
+        d_bytes = keep.tile([P, H], U8, name="d_bytes", align_bytes=64)
         nc.vector.tensor_copy(
-            d_bytes_dealt[:].rearrange("p (t c i) -> p c t i", t=PACK, i=16),
+            d_bytes[:].rearrange("p (t c i) -> p c t i", t=PACK, i=16),
             d_bytes_listed[:].rearrange("p (c i t) -> p c t i", t=PACK, i=16),
         )
-        for s in range(4):
-            nc.scalar.dma_start(d_bytes[s:P:32, :].bitcast(I32), d_bytes_dealt[8 * s : P : 32, :].bitcast(I32))
-
-        d_codes_listed = keep.tile([P, H], U32, name="d_codes_listed", align_bytes=64)
+        for e in range(2):
+            nc.sync.dma_start(d_bytes[2 + e : P : 32, :].bitcast(I32), d_bytes[16 + e : P : 32, :].bitcast(I32))
+        d_codes_listed = keep.tile([P, H], U32, name="d_codes_listed", tag="listed", align_bytes=64)
         nc.vector.tensor_copy(d_codes_listed[:], d_word_table[:].indirect(k1_sb[:]))
         d_codes = keep.tile([P, H], U32, name="d_codes", align_bytes=64)
         nc.vector.tensor_copy(
             d_codes[:].rearrange("p (t c i) -> p c t i", t=PACK, i=4),
             d_codes_listed[:].rearrange("p (c i t) -> p c t i", t=PACK, i=4),
         )
+        xq_bytes = keep.tile([P, S], U8, name="xq_bytes", tag="listed", align_bytes=64)
+        nc.vector.tensor_copy(xq_bytes[:], x_byte_table[:].indirect(offs_sb[:]))
         xq_codes = keep.tile([P, S], U32, name="xq_codes", align_bytes=64)
         nc.vector.tensor_copy(xq_codes[:], x_word_table[:].indirect(offs_sb[:]))
-        xq_bytes = keep.tile([P, S], U8, name="xq_bytes", align_bytes=64)
-        nc.vector.tensor_copy(xq_bytes[:], x_byte_table[:].indirect(offs_sb[:]))
         xc_bytes = keep.tile([P, C], U8, name="xc_bytes", align_bytes=64)
         nc.vector.tensor_copy(xc_bytes[:], x_byte_table[:].indirect(cand_sb[:]))
         xc_codes = keep.tile([P, C], U32, name="xc_codes", align_bytes=64)
@@ -144,12 +142,11 @@ def tile_picked_pqcand_none_p_kernel(tc, x_words, x_scales, d_words, d_scales, g
             for b, acc in enumerate(s_acc[u]):
                 staged = keep.tile([P, per_bank, n], F32, name=f"staged{u}_{b}")
                 target = out_tiles[:, b * per_bank : (b + 1) * per_bank, j0 : j0 + n]
-                if b == 0 or u < len(CHUNKS) - 1:
+                if b % 2 == 0 or u < len(CHUNKS) - 1:
                     nc.scalar.activation(staged[:], acc[:], COPY, scale=0.0625)
-                    nc.sync.dma_start(target, staged[:])
                 else:
                     nc.vector.tensor_scalar(staged[:], acc[:], 0.0625, None, ALU.mult)
-                    nc.scalar.dma_start(target, staged[:])
+                nc.sync.dma_start(target, staged[:])
 
         for t in range(PACK):
             cols = slice(t * P, (t + 1) * P)

from contextlib import ExitStack

import concourse.mybir as mybir

K, T, S, G, H, C = 512, 2048, 512, 2048, 512, 512
FLOPS = 2 * K * H * S + 2 * K * C * S

F32 = mybir.dt.float32
BF16 = mybir.dt.bfloat16
I32 = mybir.dt.int32
U32 = mybir.dt.uint32
U16 = mybir.dt.uint16
U8 = mybir.dt.uint8
FP8X4 = mybir.dt.float8_e4m3fn_x4
ALU = mybir.AluOpType
COPY = mybir.ActivationFunctionType.Copy

P = 128
PACK = 4
D_FIRST = 1024
CLEAR_SPLIT = 1280
CHUNKS = [256, 128, 128]
BANKS = [["s0", "s1"], ["s2"], ["s3", "h0", "h1", "h2"]]
TAIL_SCALAR = 48


def tile_picked_pqcand_none_p_kernel(tc, x_words, x_scales, d_words, d_scales, gs, offs, k1, nb, cand, out):
    nc = tc.nc
    with ExitStack() as ctx:
        keep = ctx.enter_context(tc.tile_pool(name="keep", bufs=1))
        psum = ctx.enter_context(tc.psum_pool(name="psum", bufs=1))

        k1_sb = keep.tile([P, H // 16], U16, name="k1_sb")
        offs_sb = keep.tile([P, S // 16], U16, name="offs_sb")
        cand_sb = keep.tile([P, C // 16], U16, name="cand_sb")
        nb_sb = keep.tile([P, S // 16], U16, name="nb_sb")
        d_word_table = keep.tile([P, G], U32, name="d_word_table", align_bytes=64)
        x_word_table = keep.tile([P, T], U32, name="x_word_table", align_bytes=64)
        d_byte_table = keep.tile([P, G], U8, name="d_byte_table", align_bytes=64)
        x_byte_table = keep.tile([P, T], U8, name="x_byte_table", align_bytes=64)
        gain = keep.tile([P, PACK], F32, name="gain")

        for table in (d_byte_table, x_byte_table):
            nc.vector.memset(table[:, :CLEAR_SPLIT].bitcast(I32), 0)
            nc.gpsimd.memset(table[:, CLEAR_SPLIT:].bitcast(I32), 0)

        d_rows = d_words[0].rearrange("p n t -> p (n t)").bitcast(I32)
        nc.sync.dma_start(k1_sb[:], k1)
        for e in range(2):
            nc.scalar.dma_start(d_byte_table[e:P:16, :].bitcast(I32), d_scales[0, e:16:2, :].bitcast(I32))
        nc.sync.dma_start(offs_sb[:], offs)
        nc.sync.dma_start(nb_sb[:], nb)
        nc.sync.dma_start(gain[:], gs.rearrange("(p t) o -> p (t o)", t=PACK))
        nc.sync.dma_start(d_word_table[:, :D_FIRST].bitcast(I32), d_rows[:, :D_FIRST])
        nc.sync.dma_start(d_word_table[:, D_FIRST:].bitcast(I32), d_rows[:, D_FIRST:])
        for s in range(4):
            nc.scalar.dma_start(x_byte_table[s:P:32, :].bitcast(I32), x_scales[0, s:16:4, :].bitcast(I32))
        nc.sync.dma_start(x_word_table[:].bitcast(I32), x_words[0].rearrange("p n t -> p (n t)").bitcast(I32))
        nc.sync.dma_start(cand_sb[:], cand)

        d_bytes_listed = keep.tile([P, H], U8, name="d_bytes_listed", align_bytes=64)
        nc.vector.tensor_copy(d_bytes_listed[:], d_byte_table[:].indirect(k1_sb[:]))
        d_bytes = keep.tile([P, H], U8, name="d_bytes", align_bytes=64)
        nc.vector.tensor_copy(
            d_bytes[:].rearrange("p (t c i) -> p c t i", t=PACK, i=16),
            d_bytes_listed[:].rearrange("p (c i t) -> p c t i", t=PACK, i=16),
        )
        for e in range(2):
            nc.sync.dma_start(d_bytes[2 + e : P : 32, :].bitcast(I32), d_bytes[16 + e : P : 32, :].bitcast(I32))
        d_codes_listed = keep.tile([P, H], U32, name="d_codes_listed", tag="listed", align_bytes=64)
        nc.vector.tensor_copy(d_codes_listed[:], d_word_table[:].indirect(k1_sb[:]))
        d_codes = keep.tile([P, H], U32, name="d_codes", align_bytes=64)
        nc.vector.tensor_copy(
            d_codes[:].rearrange("p (t c i) -> p c t i", t=PACK, i=4),
            d_codes_listed[:].rearrange("p (c i t) -> p c t i", t=PACK, i=4),
        )
        xq_bytes = keep.tile([P, S], U8, name="xq_bytes", tag="listed", align_bytes=64)
        nc.vector.tensor_copy(xq_bytes[:], x_byte_table[:].indirect(offs_sb[:]))
        xq_codes = keep.tile([P, S], U32, name="xq_codes", align_bytes=64)
        nc.vector.tensor_copy(xq_codes[:], x_word_table[:].indirect(offs_sb[:]))
        xc_bytes = keep.tile([P, C], U8, name="xc_bytes", align_bytes=64)
        nc.vector.tensor_copy(xc_bytes[:], x_byte_table[:].indirect(cand_sb[:]))
        xc_codes = keep.tile([P, C], U32, name="xc_codes", align_bytes=64)
        nc.vector.tensor_copy(xc_codes[:], x_word_table[:].indirect(cand_sb[:]))

        starts = [sum(CHUNKS[:u]) for u in range(len(CHUNKS))]
        h_acc, window, own, planes, woven, s_acc = [], [], {}, {}, {}, {}
        out_tiles = out.rearrange("(m p) j -> p m j", p=P)

        def copy_own(u, t):
            own[u, t] = keep.tile([P, CHUNKS[u]], F32, name=f"own{u}_{t}")
            nc.scalar.activation(own[u, t][:], h_acc[t][:, starts[u] : starts[u] + CHUNKS[u]], COPY, scale=-0.0625)

        def fetch(u):
            n, j0 = CHUNKS[u], starts[u]
            planes[u] = keep.tile([P, PACK, n], BF16, name=f"planes{u}", align_bytes=64)
            diff = keep.tile([P, PACK, n], F32, name=f"diff{u}", tag=f"turn{u % 2}", align_bytes=64)
            for t in range(PACK + 1):
                if t < PACK:
                    nc.vector.tensor_tensor(
                        diff[:, t, :], window[t][:].indirect(nb_sb[:, j0 // 16 : (j0 + n) // 16]), own[u, t][:], ALU.subtract
                    )
                if t > 0:
                    nc.vector.tensor_scalar(planes[u][:, t - 1, :], diff[:, t - 1, :], 0.0, gain[:, t - 1 : t], ALU.max, ALU.mult)

        def weave(u):
            woven[u] = keep.tile([P, CHUNKS[u], PACK], BF16, name=f"woven{u}", tag=f"turn{u % 2}", align_bytes=64)
            n = CHUNKS[u]
            cut = n if u < len(CHUNKS) - 1 else TAIL_SCALAR
            nc.scalar.copy(
                woven[u][:, :cut, :].rearrange("p (c i) t -> p c t i", i=4),
                planes[u][:, :, :cut].rearrange("p t (c i) -> p c t i", i=4),
            )
            if cut < n:
                nc.vector.tensor_copy(
                    woven[u][:, cut:, :].rearrange("p (c i) t -> p c t i", i=4),
                    planes[u][:, :, cut:].rearrange("p t (c i) -> p c t i", i=4),
                )

        def score(u, tags):
            n = CHUNKS[u]
            z_codes = keep.tile([P, n], U32, name=f"z_codes{u}", align_bytes=64)
            z_bytes = keep.tile([P, n], U8, name=f"z_bytes{u}", align_bytes=64)
            nc.vector.quantize_mx(out=z_codes[:].bitcast(FP8X4), scales=z_bytes[:], in_=woven[u][:].rearrange("p j t -> p (j t)"))
            per_bank = C // P // len(tags)
            s_acc[u] = [psum.tile([P, per_bank, n], F32, name=f"s_acc{u}_{b}", tag=tag) for b, tag in enumerate(tags)]
            for m in range(C // P):
                cols = slice(m * P, (m + 1) * P)
                nc.tensor.matmul_mx(
                    out=s_acc[u][m // per_bank][:, m % per_bank, :],
                    lhsT=xc_codes[:, cols].bitcast(FP8X4),
                    lhsT_scale=xc_bytes[:, cols],
                    rhs=z_codes[:].bitcast(FP8X4),
                    rhs_scale=z_bytes[:],
                    start=True,
                    stop=True,
                )

        def store(u):
            n, j0 = CHUNKS[u], starts[u]
            per_bank = C // P // len(s_acc[u])
            for b, acc in enumerate(s_acc[u]):
                staged = keep.tile([P, per_bank, n], F32, name=f"staged{u}_{b}")
                target = out_tiles[:, b * per_bank : (b + 1) * per_bank, j0 : j0 + n]
                if b % 2 == 0 or u < len(CHUNKS) - 1:
                    nc.scalar.activation(staged[:], acc[:], COPY, scale=0.0625)
                else:
                    nc.vector.tensor_scalar(staged[:], acc[:], 0.0625, None, ALU.mult)
                nc.sync.dma_start(target, staged[:])

        for t in range(PACK):
            cols = slice(t * P, (t + 1) * P)
            h_acc.append(psum.tile([P, S], F32, name=f"h_acc{t}", tag=f"h{t}"))
            nc.tensor.matmul_mx(
                out=h_acc[t][:],
                lhsT=d_codes[:, cols].bitcast(FP8X4),
                lhsT_scale=d_bytes[:, cols],
                rhs=xq_codes[:].bitcast(FP8X4),
                rhs_scale=xq_bytes[:],
                start=True,
                stop=True,
            )
            window.append(keep.tile([P, S], F32, name=f"window{t}"))
            nc.scalar.activation(window[t][:], h_acc[t][:], COPY, scale=-0.0625)
            copy_own(0, t)

        last = len(CHUNKS) - 1
        for u in range(last + 3):
            if u <= last:
                fetch(u)
            if u + 1 <= last:
                for t in range(PACK):
                    copy_own(u + 1, t)
            if 1 <= u <= last + 1:
                score(u - 1, BANKS[u - 1])
            if u <= last:
                weave(u)
            if 1 <= u <= last + 1:
                store(u - 1)
